import numpy as np, ml_dtypes
CORES = [16,17,18,19,32,33,34,35]
N = 8
BF = ml_dtypes.bfloat16
def gentries(a):
    return np.ascontiguousarray(a.reshape(8, 16, -1).transpose(0, 2, 1)).reshape(8, -1)
def gtable(e):
    e = np.asarray(e); return np.ascontiguousarray(e.reshape(8, -1, 16).transpose(0, 2, 1)).reshape(128, -1).astype(np.int32)
DR, NZ, Z, R = 1, 4, 2048, 2
ND, DD, C = N * DR, N * DR - 2, 2 * Z // R
def disks(x):
    return np.ascontiguousarray(x.astype(np.float32).astype(np.int32).reshape(N, 128, DR, NZ, Z).transpose(0, 2, 3, 1, 4)).reshape(ND, NZ, 128, Z)
def turns(pi):
    return np.ascontiguousarray(np.stack([gentries(a) for a in pi]).reshape(N, 8, DR, NZ, Z).transpose(0, 2, 3, 1, 4)).reshape(ND, NZ, 8, Z)
def follow(pa, pb):
    inv = np.zeros(Z, np.int64); inv[pb] = np.arange(Z)
    return inv, pa[inv]
def solve(w, p, a, b, ze):
    ps = w[DD].copy(); qs = w[DD + 1].copy()
    for i in range(DD):
        if i != a and i != b: ps -= w[i]; qs -= w[i][:, p[i]]
    ps = np.ascontiguousarray(ps.T) & 255; qs = np.ascontiguousarray(qs.T) & 255
    inv, nx = follow(p[a], p[b]); d = ps - qs[inv]; live = (ze == 0)[:, None]; xa = np.zeros((Z, 16), np.int32)
    for s in range(128): xa = np.where(live, d + xa[nx], 0) & 255
    return xa, (ps - xa) & 255, qs
def some_bytes(rng, *shape):
    return rng.integers(0, 256, shape, dtype=np.uint8).astype(np.int32)
def some_turns(rng):
    return rng.permuted(np.tile(np.arange(Z), (DD, NZ, 8, 1)), axis=-1)
def some_pairs(rng):
    o = rng.permutation(DD); return np.array([[o[g % DD], o[(g + rng.integers(1, DD)) % DD]] for g in range(8)])
def marks(rng, nx, gaps, first):
    m = np.zeros(Z, bool); n = nx.tolist(); seen = [False] * Z; u = 0
    for s in first + rng.permutation(Z).tolist():
        left = 0
        while not seen[s]:
            seen[s] = True
            if left == 0: m[s] = True; left = gaps[u]; u += 1
            left -= 1; s = n[s]
    return m
def write(rng, v, p, lo, far=False, first=None):
    ze = np.zeros((NZ, 8, Z), bool); qs = np.zeros((NZ, 128, Z), np.int32)
    for z in range(NZ):
        for g in range(8):
            a, b = lo[g]; k = slice(16 * g, 16 * g + 16)
            gaps = np.where(rng.random(Z) < (1 if far else 0.25), 128, rng.integers(1, 129, Z)).tolist()
            ze[z, g] = marks(rng, follow(p[a, z, g], p[b, z, g])[1], gaps, [] if first is None else first[g])
            v[a, z, k] *= ~ze[z, g]
            for i in range(DD): qs[z, k] += v[i, z, k][:, p[i, z, g]]
    ps = np.add.reduce(v, axis=0)
    for g in range(8):
        for i in lo[g]: v[i, :, 16 * g:16 * g + 16] = some_bytes(rng, NZ, 16, Z)
    w = np.concatenate([v, ps[None] & 255, qs[None] & 255]); t = np.concatenate([p, np.tile(np.arange(Z), (2, NZ, 8, 1))])
    t = t.reshape(N, DR, NZ, 8, Z).transpose(0, 3, 1, 2, 4).reshape(N, 8, -1)
    return {"x": np.ascontiguousarray(w.reshape(N, DR, NZ, 128, Z).transpose(0, 3, 1, 2, 4)).reshape(N, 128, -1).astype(np.float32).astype(BF),
            "pi": np.stack([gtable(e) for e in t]), "lost": np.stack([np.repeat(lo, 16, axis=0).astype(np.int32)] * N), "zero": np.stack([gtable(ze[q // R]) for q in range(N)])}
def setup_inputs(rng):
    return write(rng, some_bytes(rng, DD, NZ, 128, Z), some_turns(rng), some_pairs(rng))
def setup_inputs_long(rng):
    p = some_turns(rng); lo = some_pairs(rng)
    for z in range(NZ):
        for g in range(8):
            o = np.arange(Z) if g == 0 else np.arange(Z)[::-1] if g == 1 else rng.permutation(Z)
            c = np.zeros(Z, np.int64); c[o] = np.roll(o, -1); a, b = lo[g]; p[a, z, g] = c[p[b, z, g]]
    return write(rng, some_bytes(rng, DD, NZ, 128, Z), p, lo, True, [[0], [Z - 1]] + [[]] * 6)
def setup_inputs_short(rng):
    p = some_turns(rng); lo = some_pairs(rng); h = rng.permutation(8)
    for z in range(NZ):
        for u in range(6):
            g = h[u]; a, b = lo[g]; o = rng.permutation(Z); c = np.arange(Z)
            if u == 1: c[o[0::2]] = o[1::2]; c[o[1::2]] = o[0::2]
            if u == 2:
                i = 0
                while i < Z:
                    n = int(rng.integers(1, 6)); k = o[i:i + n]; c[k] = np.roll(k, -1); i += n
            if u < 3: p[a, z, g] = c[p[b, z, g]]
            if u == 3:
                for i in range(DD):
                    if i != a and i != b: p[i, z, g] = np.arange(Z)
            if u == 4: p[b, z, g] = np.arange(Z)
            if u == 5: p[a, z, g] = np.arange(Z)
    return write(rng, some_bytes(rng, DD, NZ, 128, Z), p, lo, True)
def setup_inputs_pair(rng):
    lo = np.array([[0, DD - 1] if e else [DD - 1, 0] for e in rng.permutation(8) < 4])
    return write(rng, some_bytes(rng, DD, NZ, 128, Z), some_turns(rng), lo)
def setup_inputs_spread(rng):
    v = some_bytes(rng, DD, NZ, 128, Z) & rng.choice(np.array([0, 1, 3, 15, 63, 128, 255], np.int32), (DD, NZ, 1, Z))
    v[rng.random(v.shape, dtype=np.float32) < 0.2] = 255
    return write(rng, v, some_turns(rng), some_pairs(rng))
def check_inputs(d):
    bad = []; x = d["x"].astype(np.float32); p = turns(d["pi"]); lo = d["lost"]; ze = d["zero"]
    if not ((x >= 0) & (x <= 255) & (x == np.floor(x))).all(): bad.append("bytes")
    if not (np.sort(p, axis=-1) == np.arange(Z)).all(): bad.append("permutations")
    if not (p[DD:] == np.arange(Z)).all(): bad.append("identity")
    if not ((lo >= 0) & (lo < DD)).all() or not (lo[:, :, 0] != lo[:, :, 1]).all() or not (lo == np.repeat(lo[0, ::16], 16, axis=0)).all(): bad.append("lost")
    if not ((ze == 0) | (ze == 1)).all() or not all((ze[q] == ze[q - q % R]).all() for q in range(N)): bad.append("zero")
    if bad: return bad
    v = disks(d["x"])
    for z in range(NZ):
        e = gentries(ze[z * R])
        for g in range(8):
            a, b = int(lo[0, 16 * g, 0]), int(lo[0, 16 * g, 1]); nx = follow(p[a, z, g], p[b, z, g])[1]; m = e[g][nx] == 1; first = m
            for s in range(127): m = first | m[nx]
            if not m.all(): bad.append("chains")
            xa, xb, qs = solve(v[:, z, 16 * g:16 * g + 16], p[:, z, g], a, b, e[g])
            if not (((xa[p[a, z, g]] + xb[p[b, z, g]]) & 255) == qs).all(): bad.append("sums")
    return sorted(set(bad))
def reference(x, pi, lost, zero):
    v = disks(x); p = turns(pi); y = np.zeros((N, 128, C), np.float32)
    for z in range(NZ):
        e = gentries(zero[z * R])
        for g in range(8):
            xa, xb, qs = solve(v[:, z, 16 * g:16 * g + 16], p[:, z, g], int(lost[0, 16 * g, 0]), int(lost[0, 16 * g, 1]), e[g])
            both = np.concatenate([xa, xb]).T
            for s in range(R): y[z * R + s, 16 * g:16 * g + 16] = both[:, s * C:(s + 1) * C]
    return {"y": y.astype(BF)}

@@ -1,0 +1,445 @@
+from concourse.bass import DstId, RemoteDMATransfer
+from concourse.mybir import AluOpType, ActivationFunctionType
+
+OP = AluOpType
+COPY = ActivationFunctionType.Copy
+IDENT = ActivationFunctionType.Identity
+Z = 2048
+H = 1024
+SINK = 2048
+WZ = Z + 16
+NL = 90
+LISTS = ["lb", "li"] + ["nl%d" % t for t in range(7)]
+
+SCRATCH = {"ps": ("psum", [128, 4096], "float32")}
+for _names, _cols, _dt in (
+        ("xs qs", 4 * Z, "bfloat16"), ("lfp lfq lnp lnq", 4 * H, "bfloat16"), ("zm yo", Z, "bfloat16"),
+        ("dm", 768, "bfloat16"), ("zeb bm idb", 128, "bfloat16"),
+        ("pin", 512, "int32"), ("losti", 2, "int32"), ("zin i1 i3", 128, "int32"), ("i2 i2b", 16, "int32"),
+        ("i4 i4b", 4, "int32"), ("i5", 8, "int32"), ("v7", WZ, "int32"), ("fi fj", Z, "int32"),
+        ("lp", 512, "uint16"), (" ".join(LISTS) + " la", 128, "uint16"),
+        ("ph", 512, "float16"), ("lpi sa sb", 768, "float16"), ("idh", 128, "float16"),
+        ("dd ha hb rfp rfq", Z, "float16"), ("fsp fsq nsp nsq rnp rnq", H, "float16"),
+        ("lostf", 2, "float32"), ("kcol", 4, "float32"), ("rmask", 16, "float32"), ("ea eb ms mn", 8, "float32"),
+        ("iot inv invz p1 q1 vc", Z, "float32"), ("wa wb", WZ, "float32")):
+    for _n in _names.split():
+        SCRATCH[_n] = ("sbuf", [128, _cols], _dt)
+SEMAPHORES = (["l%d" % i for i in range(NL)] + ["snt", "rpi"]
+              + ["r%s%d" % (b, s) for b in ("lfp", "lfq", "lnp", "lnq") for s in range(4)]
+              + ["rrfp0", "rrfp1", "rrfq0", "rrfq1", "rrnp", "rrnq", "rv0", "rv1"] + ["r" + n for n in LISTS])
+
+
+def tracker(g, T):
+    E = {"g": g, "v": g.vector, "s": g.scalar, "t": g.tensor, "y": g.sync}
+    known = {e: {} for e in E}
+    count, waited, recs = {}, {}, {}
+    free = ["l%d" % i for i in range(NL)]
+    own = {e: [] for e in E}
+
+    def wait(e, tok):
+        sem, val, snap = tok
+        k = known[e]
+        if k.get(sem, 0) >= val:
+            return
+        E[e].wait_ge(T.sem[sem], val)
+        waited[sem] = max(waited.get(sem, 0), val)
+        k[sem] = val
+        for s, n in snap.items():
+            if k.get(s, 0) < n:
+                k[s] = n
+
+    def span(r):
+        b, a, z = r
+        return (b, a // 512 * 512, -(-z // 512) * 512) if b == "ps" else (b, a, z)
+
+    def conflicts(who, reads, writes, acc):
+        out = []
+        for r in reads:
+            b, a, z = span(r)
+            for (x, y, kind, w, tok) in recs.get(b, []):
+                if x < z and a < y and (kind == "w" or (b == "ps" and w != who)):
+                    out.append(tok)
+        for r in writes:
+            b, a, z = span(r)
+            for (x, y, kind, w, tok) in recs.get(b, []):
+                if x < z and a < y and not (w == who and (kind == "r" or acc)):
+                    out.append(tok)
+        return out
+
+    def note(reads, writes, who, tok):
+        for r in writes:
+            b, a, z = span(r)
+            recs[b] = [q for q in recs.get(b, []) if not (a <= q[0] and q[1] <= z and q[4] is not tok)] + [(a, z, "w", who, tok)]
+        for r in reads:
+            b, a, z = span(r)
+            recs.setdefault(b, []).append((a, z, "r", who, tok))
+
+    def batch(e, items, dma=False, acc=False):
+        who = "dma" if dma else e
+        ins = []
+        for fn, reads, writes in items:
+            for t in sorted(conflicts(who, reads, writes, acc), key=lambda t: -len(t[2])):
+                wait(e, t)
+            ins.append(fn())
+        done = [s for s in own[e] if known[e].get(s, 0) == count[s]]
+        if not done:
+            done = [free.pop(0)]
+            own[e].append(done[0])
+            count[done[0]] = 0
+        sem = done[0]
+        for i in ins:
+            i.then_inc(T.sem[sem], 16 if dma else 1)
+            count[sem] += 16 if dma else 1
+        tok = (sem, count[sem], dict(known[e]))
+        for fn, reads, writes in items:
+            note(reads, writes, who, tok)
+
+    def op(e, fn, reads, writes, dma=False):
+        batch(e, [(fn, reads, writes)], dma)
+
+    def landing(b, a, z, sem, val):
+        count[sem] = val
+        note([], [(b, a, z)], "remote", (sem, val, {}))
+
+    def reading(e, reads):
+        for t in conflicts(e, reads, [], False):
+            wait(e, t)
+
+    def finish(sent):
+        count["snt"] = sent
+        for s, n in count.items():
+            if waited.get(s, 0) < n:
+                g.wait_ge(T.sem[s], n)
+
+    return op, batch, landing, reading, finish
+
+
+def rank_program(g, core, T, topo):
+    rank = T.rank_of(core)
+    if rank is None:
+        return
+    C = list(T.cores)
+    V, S, PE = g.vector, g.scalar, g.tensor
+    op, batch, landing, reading, finish = tracker(g, T)
+    local = [r for r in range(8) if topo.chip(C[r]) == topo.chip(core)]
+    l = local.index(rank)
+    near = sorted({r // 2 for r in local})
+    far = [z for z in range(4) if z not in near]
+    isA = rank % 2 == 0
+    zone, half = rank // 2, rank % 2
+    data = rank < 6
+    hasP = [s for s in range(4) if local[s] != 7]
+    hasQ = [s for s in range(4) if local[s] != 6]
+    others = [d for d in range(4) if d != l]
+    sent = [0]
+
+    def bits(es):
+        return sum(1 << e for e in es)
+
+    def R(b, a=0, z=None):
+        return (b, a, SCRATCH[b][1][1] if z is None else z)
+
+    def send(r, sem, dst, src, reads, es=None):
+        reading("g", reads)
+        a = topo.addr(C[r])
+        es = topo.engines(core, C[r]) if es is None else es
+        g.remote_dma(out_ap=dst, in_ap=src, remote_sem=T.sem[sem], local_sem=T.sem["snt"], pid=a[1], routing_id=a[0],
+                     dma_engine_mask=bits(es))
+        sent[0] += len(es)
+
+    def send_all(parts, reads):
+        reading("g", reads)
+        trs = []
+        for r, sem, dst, src, es in parts:
+            a = topo.addr(C[r])
+            trs.append(RemoteDMATransfer(dst_ids=[DstId(rid=a[0], pnc=a[1])], dma_engine_mask=bits(es),
+                                         remote_sem=T.sem[sem], src=src, dst=dst))
+            sent[0] += len(es)
+        g.remote_dma_fused(trs, local_sem=T.sem["snt"])
+
+    def width(r):
+        return len(topo.engines(C[r], core))
+    for b, who in (("lfp", hasP), ("lfq", hasQ), ("lnp", hasP), ("lnq", hasQ)):
+        for s in who:
+            if s != l:
+                landing(b, s * H, (s + 1) * H, "r%s%d" % (b, s), 4)
+    if isA:
+        landing("lpi", 0, 768, "rpi", 4 * (5 if data else 6))
+        for c in range(2):
+            landing("v7", c * H, (c + 1) * H, "rv%d" % c, width(rank + 1))
+    else:
+        for n in LISTS:
+            landing(n, 0, 128, "r" + n, width(rank - 1))
+        for b in ("rnp", "rnq"):
+            landing(b, 0, H, "r" + b, width(rank - 1))
+        away = [r for r in range(8) if r not in local]
+        for b in ("rfp", "rfq"):
+            for h in range(2):
+                landing(b, h * H, (h + 1) * H, "r%s%d" % (b, h), width(away[0]))
+
+    def load(e, dst, src, w):
+        q = g.sync if e == "y" else S
+        op(e, lambda: q.dma_start(dst, src), [], [w], True)
+
+    def loadx(e, z):
+        load(e, T.xs[:, z * Z:(z + 1) * Z], T.x[:, z * Z:(z + 1) * Z], R("xs", z * Z, (z + 1) * Z))
+    if data:
+        load("y", T.pin[:], T.pi[:], R("pin"))
+    load("s", T.losti[:], T.lost[:], R("losti"))
+    loadx("y", far[0])
+    loadx("s", far[1])
+    if isA:
+        load("s", T.zin[:], T.zero[:], R("zin"))
+    loadx("y", near[0])
+    loadx("y", near[1])
+
+    def iota(b, pattern, base, cm, **kw):
+        op("g", lambda: g.iota(T[b][:], pattern, base, cm, **kw), [], [R(b)])
+    iota("i1", [[-1, 128]], 0, 1)
+    iota("i5", [[1, 8]], 0, 0)
+    if isA:
+        iota("i2", [[-1, 16]], 16, 1)
+        iota("i3", [[1, 8], [0, 16]], 0, 0)
+        iota("i4", [[0, 4]], 0, 1)
+        iota("iot", [[1, Z]], 0, 0, allow_small_or_imprecise_dtypes=True)
+
+    def ts(out, in0, s1, s2, op0, op1, reads, writes):
+        a = (out, in0, s1, s2, op0) if op1 is None else (out, in0, s1, s2, op0, op1)
+        op("v", lambda: V.tensor_scalar(*a), reads, writes)
+
+    def tt(out, in0, in1, o, reads, writes):
+        op("v", lambda: V.tensor_tensor(out, in0, in1, o), reads, writes)
+
+    def cp(out, in_, reads, writes):
+        op("v", lambda: V.tensor_copy(out, in_), reads, writes)
+
+    def fill(b, c):
+        op("v", lambda: V.memset(T[b][:, Z:WZ], c), [], [(b, Z, WZ)])
+
+    def scaled(n, dst, idn, col):
+        items = []
+        for i in range(n):
+            b, j = col(i)
+            items.append((lambda i=i, b=b, j=j: V.tensor_scalar(T[dst][:, i * 128:(i + 1) * 128], T[idn][:], T[b][:, j:j + 1], None, OP.mult),
+                          [R(idn), R(b)], [R(dst, i * 128, (i + 1) * 128)]))
+        batch("v", items)
+
+    ts(T.idb[:], T.i1[:], 0, None, OP.is_equal, None, [R("i1")], [R("idb")])
+    ts(T.idh[:], T.i1[:], 0, None, OP.is_equal, None, [R("i1")], [R("idh")])
+    fill("v7", 0)
+    fill("wa", float(SINK) if isA else 0.0)
+    fill("wb", float(SINK) if isA else 0.0)
+    if isA:
+        ts(T.i2b[:], T.i2[:], 15, None, OP.bitwise_and, None, [R("i2")], [R("i2b")])
+        ts(T.rmask[:], T.i2b[:], 0, None, OP.is_equal, None, [R("i2b")], [R("rmask")])
+        ts(T.i4b[:], T.i4[:], 4, None, OP.arith_shift_right, None, [R("i4")], [R("i4b")])
+        cp(T.kcol[:], T.i4b[:], [R("i4b")], [R("kcol")])
+        ts(T.bm[:], T.i3[:], T.kcol[:, 0:1], float(SINK), OP.is_equal, OP.mult, [R("i3"), R("kcol")], [R("bm")])
+    cp(T.lostf[:], T.losti[:], [R("losti")], [R("lostf")])
+    ts(T.ea[:], T.i5[:], T.lostf[:, 0:1], None, OP.is_equal, None, [R("i5"), R("lostf")], [R("ea")])
+    ts(T.eb[:], T.i5[:], T.lostf[:, 1:2], None, OP.is_equal, None, [R("i5"), R("lostf")], [R("eb")])
+    tt(T.ms[:], T.ea[:], T.eb[:], OP.add, [R("ea"), R("eb")], [R("ms")])
+    ts(T.mn[:], T.ms[:], -1.0, None, OP.add, None, [R("ms")], [R("mn")])
+    if data:
+        cp(T.ph[:], T.pin[:], [R("pin")], [R("ph")])
+        cp(T.lp[:], T.pin[:], [R("pin")], [R("lp")])
+        offs = [2 * z for z in far]
+        ons = [2 * z for z in near if 2 * z != rank]
+        lo = topo.engines(core, C[offs[0]])
+        hi = [e for e in topo.engines(core, C[local[others[0]]]) if e not in lo]
+        where = [(r, lo[4 * i:4 * i + 4]) for i, r in enumerate(offs)] + [(r, hi[4 * i:4 * i + 4]) for i, r in enumerate(ons)]
+        send_all([(r, "rpi", T.lpi[:, rank * 128:(rank + 1) * 128], T.ph[:, (r // 2) * 128:(r // 2 + 1) * 128], es)
+                  for r, es in where], [R("ph")])
+    scaled(len([r for r in local if r < 6]), "dm", "idb", lambda i: ("mn", local[i]))
+
+    def weight(s):
+        return (T.dm[:, s * 128:(s + 1) * 128], R("dm", s * 128, (s + 1) * 128)) if local[s] < 6 else (T.idb[:], R("idb"))
+
+    def pick(e, dst, d0, src, s0, s1, lst, t0, n):
+        out, in_ = T[dst][:, d0:d0 + n], T[src][:, s0:s1].indirect(T[lst][:, t0:t0 + n // 16])
+        rd, wr = [R(src, s0, s1), R(lst, t0, t0 + n // 16)], [R(dst, d0, d0 + n)]
+        if e == "v":
+            op("v", lambda: V.tensor_copy(out, in_), rd, wr)
+        else:
+            op("s", lambda: S.activation(out, in_, COPY), rd, wr)
+
+    def gather(e, z):
+        pick(e, "qs", z * Z, "xs", z * Z, (z + 1) * Z, "lp", z * 128, Z)
+
+    def pieces(zs, srcb, landb, shift):
+        parts, rd = [], []
+        for i, d in enumerate(others):
+            a = zs[d // 2] * Z + d % 2 * H
+            es = topo.engines(core, C[local[d]])
+            parts.append((local[d], "r%s%d" % (landb, l), T[landb][:, l * H:(l + 1) * H], T[srcb][:, a:a + H],
+                          es[4 * (i + shift):4 * (i + shift) + 4]))
+            rd.append(R(srcb, a, a + H))
+        send_all(parts, rd)
+
+    qsrc = "qs" if data else "xs"
+    if data:
+        gather("v", far[0])
+        gather("s", far[1])
+    if l in hasP:
+        pieces(far, "xs", "lfp", 0)
+    if l in hasQ:
+        pieces(far, qsrc, "lfq", 0)
+    if l in hasP:
+        pieces(near, "xs", "lnp", 1)
+    if isA:
+        cp(T.zeb[:], T.zin[:], [R("zin")], [R("zeb")])
+        batch("s", [(lambda p=p: S.activation(T.zm[:, p:Z:16], T.zeb[:], COPY, scale=T.rmask[:, p:p + 1]),
+                     [R("zeb"), R("rmask")], [R("zm")]) for p in range(16)], acc=True)
+        scaled(6, "sb", "idh", lambda i: ("eb", i))
+        scaled(6, "sa", "idh", lambda i: ("ea", i))
+    if data:
+        gather("s", near[0])
+        gather("s" if isA else "v", near[1])
+    if l in hasQ:
+        pieces(near, qsrc, "lnq", 1)
+
+    def addup(zs, srcb, landb, who, bank, last):
+        items = []
+        seq = [s for s in who if s == l] + [s for s in who if s != l]
+        for n, s in enumerate(seq):
+            w, wr = weight(s)
+            for b in range(2):
+                buf, a = (srcb, zs[l // 2] * Z + l % 2 * H + 512 * b) if s == l else (landb, s * H + 512 * b)
+                o = (bank + b) * 512
+                items.append((lambda o=o, w=w, buf=buf, a=a, st=n == 0, en=last and n == len(seq) - 1:
+                              PE.matmul(T.ps[:, o:o + 512], w, T[buf][:, a:a + 512], st, en),
+                              [wr, R(buf, a, a + 512)], [R("ps", o, o + 512)]))
+        batch("t", items, acc=True)
+
+    def evac(dst, bank):
+        for b in range(2):
+            o = (bank + b) * 512
+            cp(T[dst][:, b * 512:b * 512 + 512], T.ps[:, o:o + 512], [R("ps", o, o + 512)], [R(dst, b * 512, b * 512 + 512)])
+
+    def far_send(src, dst):
+        h = l % 2
+        send(2 * far[l // 2] + 1, "r%s%d" % (dst, h), T[dst][:, h * H:(h + 1) * H], T[src][:], [R(src)])
+
+    def store(c0, c1):
+        op("y", lambda: g.sync.dma_start(T.y[:, c0:c1], T.yo[:, c0:c1]), [R("yo", c0, c1)], [], True)
+
+    if isA:
+        B = rank + 1
+        addup(far, "xs", "lfp", hasP, 0, True)
+        for nm, dst, o in (("sb", "lb", 2048), ("sa", "la", 2560)):
+            items = []
+            for i in range(6):
+                buf, a = ("ph", zone * 128) if i == rank else ("lpi", i * 128)
+                items.append((lambda i=i, buf=buf, a=a: PE.matmul(T.ps[:, o:o + 128], T[nm][:, i * 128:(i + 1) * 128], T[buf][:, a:a + 128], i == 0, i == 5),
+                              [R(nm, i * 128, (i + 1) * 128), R(buf, a, a + 128)], [R("ps", o, o + 128)]))
+            batch("t", items, acc=True)
+            cp(T[dst][:], T.ps[:, o:o + 128], [R("ps", o, o + 128)], [R(dst)])
+        addup(far, qsrc, "lfq", hasQ, 2, True)
+        for b in range(4):
+            o = 2048 + 512 * b
+            op("t", lambda: PE.matmul(T.ps[:, o:o + 512], T.bm[:], T.zm[:, b * 512:(b + 1) * 512], True, True),
+               [R("bm"), R("zm", b * 512, (b + 1) * 512)], [R("ps", o, o + 512)])
+
+        def scat(h):
+            cp(T.inv[:, 0:Z].indirect(T.lb[:, h * 64:(h + 1) * 64]), T.iot[:, h * H:(h + 1) * H], [R("lb"), R("iot")], [R("inv")])
+        scaled(16, "dd", "idh", lambda r: ("rmask", r))
+        scat(0)
+        evac("fsp", 0)
+        evac("fsq", 2)
+        far_send("fsp", "rfp")
+        far_send("fsq", "rfq")
+        send(B, "rlb", T.lb[:], T.lb[:], [R("lb")])
+        addup(near, "xs", "lnp", hasP, 0, True)
+        addup(near, qsrc, "lnq", hasQ, 2, True)
+        scat(1)
+        for b in range(4):
+            o, c0, c1 = 2048 + 512 * b, 512 * b, 512 * b + 512
+            tt(T.invz[:, c0:c1], T.inv[:, c0:c1], T.ps[:, o:o + 512], OP.max, [R("inv", c0, c1), R("ps", o, o + 512)], [R("invz", c0, c1)])
+
+        def totable(hbuf, src, lst):
+            for h in range(2):
+                c0, c1, o = h * H, (h + 1) * H, 2048 + 512 * h
+                cp(T[hbuf][:, c0:c1], T[src][:, c0:c1], [R(src, c0, c1)], [R(hbuf, c0, c1)])
+                batch("t", [(lambda r=r: PE.matmul(T.ps[:, o:o + 64], T.dd[:, r * 128:(r + 1) * 128], T[hbuf][:, c0 + r:c1:16], r == 0, r == 15),
+                             [R("dd", r * 128, (r + 1) * 128), R(hbuf, c0, c1)], [R("ps", o, o + 64)]) for r in range(16)], acc=True)
+                cp(T[lst][:, h * 64:(h + 1) * 64], T.ps[:, o:o + 64], [R("ps", o, o + 64)], [R(lst, h * 64, (h + 1) * 64)])
+
+        for t in range(7):
+            w, old = ("wa", "wb")[t % 2], ("wb", "wa")[t % 2]
+            src, ww, lst = ("invz", Z, "la") if t == 0 else (old, WZ, "nl%d" % (t - 1))
+            for e, c, n in (("v", 0, 512), ("s", 512, 512), ("s", 1024, 1024)):
+                pick(e, w, c, src, 0, ww, lst, c // 16, n)
+            totable(("ha", "hb")[t % 2], w, "nl%d" % t)
+            send(B, "rnl%d" % t, T["nl%d" % t][:], T["nl%d" % t][:], [R("nl%d" % t)])
+            if t == 0:
+                evac("nsp", 0)
+                evac("nsq", 2)
+                send(B, "rrnp", T.rnp[:], T.nsp[:], [R("nsp")])
+                send(B, "rrnq", T.rnq[:], T.nsq[:], [R("nsq")])
+        totable("hb", "invz", "li")
+        send(B, "rli", T.li[:], T.li[:], [R("li")])
+        for c in range(2):
+            c0, c1 = c * H, (c + 1) * H
+            ts(T.fi[:, c0:c1], T.v7[:, 0:WZ].indirect(T.li[:, c * 64:(c + 1) * 64]), 255, None, OP.bitwise_and, None,
+               [R("v7"), R("li", c * 64, (c + 1) * 64)], [R("fi", c0, c1)])
+            cp(T.yo[:, c0:c1], T.fi[:, c0:c1], [R("fi", c0, c1)], [R("yo", c0, c1)])
+            store(c0, c1)
+    else:
+        addup(far, "xs", "lfp", hasP, 0, True)
+        addup(far, qsrc, "lfq", hasQ, 2, True)
+        evac("fsp", 0)
+        evac("fsq", 2)
+        far_send("fsp", "rfp")
+        far_send("fsq", "rfq")
+        addup(near, "xs", "lnp", hasP, 4, False)
+        addup(near, qsrc, "lnq", hasQ, 6, False)
+
+        def more(buf, a, bank, st, en):
+            items = []
+            for b in range(2):
+                o, c = (bank + b) * 512, a + 512 * b
+                items.append((lambda o=o, c=c: PE.matmul(T.ps[:, o:o + 512], T.idh[:], T[buf][:, c:c + 512], st, en),
+                              [R("idh"), R(buf, c, c + 512)], [R("ps", o, o + 512)]))
+            batch("t", items, acc=True)
+
+        def settle(dst, h, bank):
+            for b in range(2):
+                o, c0 = (bank + b) * 512, h * H + 512 * b
+                rd, wr = [R("ps", o, o + 512)], [R(dst, c0, c0 + 512)]
+                if h == 0:
+                    op("s", lambda: S.activation(T[dst][:, c0:c0 + 512], T.ps[:, o:o + 512], IDENT, bias=1.0), rd, wr)
+                else:
+                    ts(T[dst][:, c0:c0 + 512], T.ps[:, o:o + 512], 1.0, None, OP.add, None, rd, wr)
+
+        more("rnp", 0, 0, True, False)
+        more("rnq", 0, 2, True, False)
+        for fb, bank, dst in (("rfp", 0, "p1"), ("rfq", 2, "q1")):
+            for h in range(2):
+                more(fb, h * H, bank + 4 * h, False, True)
+                settle(dst, h, bank + 4 * h)
+
+        def comb(dst, win, ww, lst, add, c, o):
+            c0, c1 = c * H, (c + 1) * H
+            tt(T[dst][:, c0:c1], T[win][:, 0:ww].indirect(T[lst][:, c * 64:(c + 1) * 64]), T[add][:, c0:c1], o,
+               [R(win, 0, ww), R(lst), R(add, c0, c1)], [R(dst, c0, c1)])
+
+        for t in range(7):
+            w, old = ("wa", "wb")[t % 2], ("wb", "wa")[t % 2]
+            for c in range(2):
+                if t == 0:
+                    comb(w, "p1", Z, "lb", "q1", c, OP.subtract)
+                else:
+                    comb(w, old, WZ, "nl%d" % (t - 1), "vc", c, OP.add)
+                c0, c1 = c * H, (c + 1) * H
+                op("s", lambda: S.activation(T.vc[:, c0:c1], T[w][:, c0:c1], COPY), [R(w, c0, c1)], [R("vc", c0, c1)])
+        for c in range(2):
+            c0, c1 = c * H, (c + 1) * H
+            comb("v7", "wa", WZ, "nl6", "vc", c, OP.add)
+            send(rank - 1, "rv%d" % c, T.v7[:, c0:c1], T.v7[:, c0:c1], [R("v7", c0, c1)])
+        for c in range(2):
+            c0, c1 = c * H, (c + 1) * H
+            comb("fi", "v7", WZ, "li", "p1", c, OP.subtract)
+            ts(T.fj[:, c0:c1], T.fi[:, c0:c1], 255, None, OP.bitwise_and, None, [R("fi", c0, c1)], [R("fj", c0, c1)])
+            ts(T.yo[:, c0:c1], T.fj[:, c0:c1], -1.0, 255.0, OP.mult, OP.add, [R("fj", c0, c1)], [R("yo", c0, c1)])
+            store(c0, c1)
+    finish(sent[0])

@@ -6,27 +6,28 @@ COPY = ActivationFunctionType.Copy
 IDENT = ActivationFunctionType.Identity
 Z = 2048
 H = 1024
-SINK = 2048
-WZ = Z + 16
+WZ = Z + 256
 NL = 90
 LISTS = ["lb", "li"] + ["nl%d" % t for t in range(7)]
+CH = ((1024, 2048), (0, 512), (512, 1024))
 
 SCRATCH = {"ps": ("psum", [128, 4096], "float32")}
 for _names, _cols, _dt in (
-        ("xs qs", 4 * Z, "bfloat16"), ("lfp lfq lnp lnq", 4 * H, "bfloat16"), ("zm yo", Z, "bfloat16"),
-        ("dm", 768, "bfloat16"), ("zeb bm idb", 128, "bfloat16"),
+        ("xs qs", 4 * Z, "bfloat16"), ("lfp lfq lnp", 4 * H, "bfloat16"), ("lnq", 4 * Z, "bfloat16"),
+        ("zm yo dd iot inv invz", Z, "bfloat16"),
+        ("dm dp", 512, "bfloat16"), ("zeb bm bz base idb idn", 128, "bfloat16"), ("na nb", WZ, "bfloat16"), ("il", 256, "bfloat16"),
         ("pin", 512, "int32"), ("losti", 2, "int32"), ("zin i1 i3", 128, "int32"), ("i2 i2b", 16, "int32"),
-        ("i4 i4b", 4, "int32"), ("i5", 8, "int32"), ("v7", WZ, "int32"), ("fi fj", Z, "int32"),
+        ("i4 i4b i4c", 4, "int32"), ("i5", 8, "int32"), ("v7 fi", WZ, "int32"), ("fj", Z, "int32"),
         ("lp", 512, "uint16"), (" ".join(LISTS) + " la", 128, "uint16"),
         ("ph", 512, "float16"), ("lpi sa sb", 768, "float16"), ("idh", 128, "float16"),
-        ("dd ha hb rfp rfq", Z, "float16"), ("fsp fsq nsp nsq rnp rnq", H, "float16"),
-        ("lostf", 2, "float32"), ("kcol", 4, "float32"), ("rmask", 16, "float32"), ("ea eb ms mn", 8, "float32"),
-        ("iot inv invz p1 q1 vc", Z, "float32"), ("wa wb", WZ, "float32")):
+        ("rfp rfq", Z, "float16"), ("fsp fsq relay", H, "float16"), ("nsp rnp", H, "float32"),
+        ("lostf", 2, "float32"), ("kcol odd even wcol", 4, "float32"), ("rmask", 16, "float32"), ("ea eb ms mn mp bev", 8, "float32"),
+        ("p1 q1 vc", Z, "float32"), ("wa wb", WZ, "float32")):
     for _n in _names.split():
         SCRATCH[_n] = ("sbuf", [128, _cols], _dt)
-SEMAPHORES = (["l%d" % i for i in range(NL)] + ["snt", "rpi"]
+SEMAPHORES = (["l%d" % i for i in range(NL)] + ["snt", "rpi", "rrelay"]
               + ["r%s%d" % (b, s) for b in ("lfp", "lfq", "lnp", "lnq") for s in range(4)]
-              + ["rrfp0", "rrfp1", "rrfq0", "rrfq1", "rrnp", "rrnq", "rv0", "rv1"] + ["r" + n for n in LISTS])
+              + ["rrfp0", "rrfp1", "rrfq0", "rrfq1", "rrnp", "rv0", "rv1", "rv2"] + ["r" + n for n in LISTS])
 
 
 def tracker(g, T):
@@ -114,11 +115,32 @@ def tracker(g, T):
     return op, batch, landing, reading, finish
 
 
+def bits(es):
+    return sum(1 << e for e in es)
+
+
+def relay_of(core, T, topo):
+    cs = topo.cores_of(core)
+    same = [c for c in cs if T.rank_of(c) is not None and topo.die(c) == topo.die(core)]
+    free = [c for c in cs if T.rank_of(c) is None and topo.die(c) != topo.die(core)]
+    return free[same.index(core)]
+
+
 def rank_program(g, core, T, topo):
     rank = T.rank_of(core)
-    if rank is None:
-        return
     C = list(T.cores)
+    if rank is None:
+        for c in C[0::2]:
+            if topo.chip(c) == topo.chip(core) and relay_of(c, T, topo) == core:
+                here = [d for d in C if topo.chip(d) == topo.chip(c)]
+                zs = [z for z in range(4) if C[2 * z] not in here]
+                to = C[2 * zs[here.index(c) // 2] + 1]
+                a = topo.addr(to)
+                g.wait_ge(T.sem["rrelay"], len(topo.engines(c, to)))
+                g.remote_dma(out_ap=T.rfp[:, 0:H], in_ap=T.relay[:], remote_sem=T.sem["rrfp0"],
+                             local_sem=T.sem["snt"], pid=a[1], routing_id=a[0], dma_engine_mask=topo.mask(core, to))
+                g.wait_ge(T.sem["snt"], len(topo.engines(core, to)))
+        return
     V, S, PE = g.vector, g.scalar, g.tensor
     op, batch, landing, reading, finish = tracker(g, T)
     local = [r for r in range(8) if topo.chip(C[r]) == topo.chip(core)]
@@ -126,23 +148,24 @@ def rank_program(g, core, T, topo):
     near = sorted({r // 2 for r in local})
     far = [z for z in range(4) if z not in near]
     isA = rank % 2 == 0
-    zone, half = rank // 2, rank % 2
+    zone = rank // 2
     data = rank < 6
     hasP = [s for s in range(4) if local[s] != 7]
     hasQ = [s for s in range(4) if local[s] != 6]
     others = [d for d in range(4) if d != l]
+    away = [r for r in range(8) if r not in local]
+    all_es = topo.engines(core, C[local[others[0]]])
+    off_es = topo.engines(core, C[away[0]])
+    on_es = [e for e in all_es if e not in off_es]
     sent = [0]
-
-    def bits(es):
-        return sum(1 << e for e in es)
 
     def R(b, a=0, z=None):
         return (b, a, SCRATCH[b][1][1] if z is None else z)
 
-    def send(r, sem, dst, src, reads, es=None):
+    def send(to, sem, dst, src, reads, es=None):
         reading("g", reads)
-        a = topo.addr(C[r])
-        es = topo.engines(core, C[r]) if es is None else es
+        a = topo.addr(to)
+        es = topo.engines(core, to) if es is None else es
         g.remote_dma(out_ap=dst, in_ap=src, remote_sem=T.sem[sem], local_sem=T.sem["snt"], pid=a[1], routing_id=a[0],
                      dma_engine_mask=bits(es))
         sent[0] += len(es)
@@ -159,20 +182,18 @@ def rank_program(g, core, T, topo):
 
     def width(r):
         return len(topo.engines(C[r], core))
-    for b, who in (("lfp", hasP), ("lfq", hasQ), ("lnp", hasP), ("lnq", hasQ)):
+    for b, who, w, n in (("lfp", hasP, H, 4), ("lfq", hasQ, H, 4), ("lnp", hasP, H, len(on_es)), ("lnq", hasQ, Z, len(all_es))):
         for s in who:
-            if s != l:
-                landing(b, s * H, (s + 1) * H, "r%s%d" % (b, s), 4)
+            if s != l and not (isA and b == "lnq"):
+                landing(b, s * w, (s + 1) * w, "r%s%d" % (b, s), n)
     if isA:
         landing("lpi", 0, 768, "rpi", 4 * (5 if data else 6))
-        for c in range(2):
-            landing("v7", c * H, (c + 1) * H, "rv%d" % c, width(rank + 1))
+        for c, (c0, c1) in enumerate(CH):
+            landing("v7", c0, c1, "rv%d" % c, width(rank + 1))
     else:
         for n in LISTS:
             landing(n, 0, 128, "r" + n, width(rank - 1))
-        for b in ("rnp", "rnq"):
-            landing(b, 0, H, "r" + b, width(rank - 1))
-        away = [r for r in range(8) if r not in local]
+        landing("rnp", 0, H, "rrnp", width(rank - 1))
         for b in ("rfp", "rfq"):
             for h in range(2):
                 landing(b, h * H, (h + 1) * H, "r%s%d" % (b, h), width(away[0]))
@@ -183,15 +204,16 @@ def rank_program(g, core, T, topo):
 
     def loadx(e, z):
         load(e, T.xs[:, z * Z:(z + 1) * Z], T.x[:, z * Z:(z + 1) * Z], R("xs", z * Z, (z + 1) * Z))
+    mine_first = sorted(near, key=lambda z: z != zone)
     if data:
         load("y", T.pin[:], T.pi[:], R("pin"))
     load("s", T.losti[:], T.lost[:], R("losti"))
-    loadx("y", far[0])
-    loadx("s", far[1])
     if isA:
         load("s", T.zin[:], T.zero[:], R("zin"))
-    loadx("y", near[0])
-    loadx("y", near[1])
+    loadx("y", far[0])
+    loadx("s", far[1])
+    for z in mine_first:
+        loadx("y", z)
 
     def iota(b, pattern, base, cm, **kw):
         op("g", lambda: g.iota(T[b][:], pattern, base, cm, **kw), [], [R(b)])
@@ -201,7 +223,7 @@ def rank_program(g, core, T, topo):
         iota("i2", [[-1, 16]], 16, 1)
         iota("i3", [[1, 8], [0, 16]], 0, 0)
         iota("i4", [[0, 4]], 0, 1)
-        iota("iot", [[1, Z]], 0, 0, allow_small_or_imprecise_dtypes=True)
+        iota("il", [[1, 256]], 0, 0, allow_small_or_imprecise_dtypes=True)
 
     def ts(out, in0, s1, s2, op0, op1, reads, writes):
         a = (out, in0, s1, s2, op0) if op1 is None else (out, in0, s1, s2, op0, op1)
@@ -213,8 +235,8 @@ def rank_program(g, core, T, topo):
     def cp(out, in_, reads, writes):
         op("v", lambda: V.tensor_copy(out, in_), reads, writes)
 
-    def fill(b, c):
-        op("v", lambda: V.memset(T[b][:, Z:WZ], c), [], [(b, Z, WZ)])
+    def fill(b, c, a=Z, z=WZ):
+        op("v", lambda: V.memset(T[b][:, a:z], c), [], [(b, a, z)])
 
     def scaled(n, dst, idn, col):
         items = []
@@ -224,36 +246,35 @@ def rank_program(g, core, T, topo):
                           [R(idn), R(b)], [R(dst, i * 128, (i + 1) * 128)]))
         batch("v", items)
 
-    ts(T.idb[:], T.i1[:], 0, None, OP.is_equal, None, [R("i1")], [R("idb")])
-    ts(T.idh[:], T.i1[:], 0, None, OP.is_equal, None, [R("i1")], [R("idh")])
-    fill("v7", 0)
-    fill("wa", float(SINK) if isA else 0.0)
-    fill("wb", float(SINK) if isA else 0.0)
     if isA:
+        fill("dd", 0.0, 0, Z)
+    ts(T.idb[:], T.i1[:], 0, None, OP.is_equal, None, [R("i1")], [R("idb")])
+    if isA:
+        ts(T.idh[:], T.i1[:], 0, None, OP.is_equal, None, [R("i1")], [R("idh")])
         ts(T.i2b[:], T.i2[:], 15, None, OP.bitwise_and, None, [R("i2")], [R("i2b")])
-        ts(T.rmask[:], T.i2b[:], 0, None, OP.is_equal, None, [R("i2b")], [R("rmask")])
         ts(T.i4b[:], T.i4[:], 4, None, OP.arith_shift_right, None, [R("i4")], [R("i4b")])
+        ts(T.i4c[:], T.i4[:], 1, None, OP.bitwise_and, None, [R("i4")], [R("i4c")])
+        ts(T.rmask[:], T.i2b[:], 0, None, OP.is_equal, None, [R("i2b")], [R("rmask")])
         cp(T.kcol[:], T.i4b[:], [R("i4b")], [R("kcol")])
-        ts(T.bm[:], T.i3[:], T.kcol[:, 0:1], float(SINK), OP.is_equal, OP.mult, [R("i3"), R("kcol")], [R("bm")])
+        cp(T.odd[:], T.i4c[:], [R("i4c")], [R("odd")])
+    if data:
+        cp(T.ph[:], T.pin[:], [R("pin")], [R("ph")])
+        where = [(2 * z, off_es[4 * i:4 * i + 4]) for i, z in enumerate(far)]
+        where += [(r, on_es[4 * i:4 * i + 4]) for i, r in enumerate(2 * z for z in near if 2 * z != rank)]
+        send_all([(r, "rpi", T.lpi[:, rank * 128:(rank + 1) * 128], T.ph[:, (r // 2) * 128:(r // 2 + 1) * 128], es)
+                  for r, es in where], [R("ph")])
+        cp(T.lp[:], T.pin[:], [R("pin")], [R("lp")])
     cp(T.lostf[:], T.losti[:], [R("losti")], [R("lostf")])
     ts(T.ea[:], T.i5[:], T.lostf[:, 0:1], None, OP.is_equal, None, [R("i5"), R("lostf")], [R("ea")])
     ts(T.eb[:], T.i5[:], T.lostf[:, 1:2], None, OP.is_equal, None, [R("i5"), R("lostf")], [R("eb")])
     tt(T.ms[:], T.ea[:], T.eb[:], OP.add, [R("ea"), R("eb")], [R("ms")])
     ts(T.mn[:], T.ms[:], -1.0, None, OP.add, None, [R("ms")], [R("mn")])
-    if data:
-        cp(T.ph[:], T.pin[:], [R("pin")], [R("ph")])
-        cp(T.lp[:], T.pin[:], [R("pin")], [R("lp")])
-        offs = [2 * z for z in far]
-        ons = [2 * z for z in near if 2 * z != rank]
-        lo = topo.engines(core, C[offs[0]])
-        hi = [e for e in topo.engines(core, C[local[others[0]]]) if e not in lo]
-        where = [(r, lo[4 * i:4 * i + 4]) for i, r in enumerate(offs)] + [(r, hi[4 * i:4 * i + 4]) for i, r in enumerate(ons)]
-        send_all([(r, "rpi", T.lpi[:, rank * 128:(rank + 1) * 128], T.ph[:, (r // 2) * 128:(r // 2 + 1) * 128], es)
-                  for r, es in where], [R("ph")])
-    scaled(len([r for r in local if r < 6]), "dm", "idb", lambda i: ("mn", local[i]))
+    nd = len([r for r in local if r < 6])
+    scaled(nd, "dm", "idb", lambda i: ("mn", local[i]))
 
-    def weight(s):
-        return (T.dm[:, s * 128:(s + 1) * 128], R("dm", s * 128, (s + 1) * 128)) if local[s] < 6 else (T.idb[:], R("idb"))
+    def weight(s, plus):
+        m, i = ("dm", "idb") if plus else ("dp", "idn")
+        return (T[m][:, s * 128:(s + 1) * 128], R(m, s * 128, (s + 1) * 128)) if local[s] < 6 else (T[i][:], R(i))
 
     def pick(e, dst, d0, src, s0, s1, lst, t0, n):
         out, in_ = T[dst][:, d0:d0 + n], T[src][:, s0:s1].indirect(T[lst][:, t0:t0 + n // 16])
@@ -266,66 +287,100 @@ def rank_program(g, core, T, topo):
     def gather(e, z):
         pick(e, "qs", z * Z, "xs", z * Z, (z + 1) * Z, "lp", z * 128, Z)
 
-    def pieces(zs, srcb, landb, shift):
-        parts, rd = [], []
-        for i, d in enumerate(others):
-            a = zs[d // 2] * Z + d % 2 * H
-            es = topo.engines(core, C[local[d]])
-            parts.append((local[d], "r%s%d" % (landb, l), T[landb][:, l * H:(l + 1) * H], T[srcb][:, a:a + H],
-                          es[4 * (i + shift):4 * (i + shift) + 4]))
-            rd.append(R(srcb, a, a + H))
-        send_all(parts, rd)
+    def piece(zs, srcb, landb, d, w, es):
+        a = zs[d // 2] * Z + (d % 2 * H if w == H else 0)
+        return (local[d], "r%s%d" % (landb, l), T[landb][:, l * w:(l + 1) * w], T[srcb][:, a:a + w], es), R(srcb, a, a + w)
+
+    def far_pieces(srcb, landb):
+        ps = [piece(far, srcb, landb, d, H, topo.engines(core, C[local[d]])[4 * i:4 * i + 4]) for i, d in enumerate(others)]
+        send_all([p[0] for p in ps], [p[1] for p in ps])
+
+    def near_pieces(srcb, landb, to, w, es):
+        for d in sorted(to, key=lambda d: d // 2 != l // 2):
+            (r, sem, dst, src, es), rd = piece(near, srcb, landb, d, w, es)
+            send(C[r], sem, dst, src, [rd], es)
 
     qsrc = "qs" if data else "xs"
     if data:
         gather("v", far[0])
         gather("s", far[1])
     if l in hasP:
-        pieces(far, "xs", "lfp", 0)
+        far_pieces("xs", "lfp")
     if l in hasQ:
-        pieces(far, qsrc, "lfq", 0)
+        far_pieces(qsrc, "lfq")
     if l in hasP:
-        pieces(near, "xs", "lnp", 1)
-    if isA:
-        cp(T.zeb[:], T.zin[:], [R("zin")], [R("zeb")])
-        batch("s", [(lambda p=p: S.activation(T.zm[:, p:Z:16], T.zeb[:], COPY, scale=T.rmask[:, p:p + 1]),
-                     [R("zeb"), R("rmask")], [R("zm")]) for p in range(16)], acc=True)
-        scaled(6, "sb", "idh", lambda i: ("eb", i))
-        scaled(6, "sa", "idh", lambda i: ("ea", i))
+        near_pieces("xs", "lnp", others, H, on_es)
+    if not isA:
+        ts(T.mp[:], T.mn[:], -1.0, None, OP.mult, None, [R("mn")], [R("mp")])
+        scaled(nd, "dp", "idb", lambda i: ("mp", local[i]))
+        ts(T.idn[:], T.idb[:], -1.0, None, OP.mult, None, [R("idb")], [R("idn")])
     if data:
-        gather("s", near[0])
-        gather("s" if isA else "v", near[1])
-    if l in hasQ:
-        pieces(near, qsrc, "lnq", 1)
+        gather("s", mine_first[0])
+        gather("s" if isA else "v", mine_first[1])
 
-    def addup(zs, srcb, landb, who, bank, last):
+    def addup(zs, srcb, landb, who, bank, mine, half=None, plus=True):
         items = []
+        z, w, d, h = (zs[l // 2], H, 0, l % 2) if half is None else (zone, Z, half * H, half)
         seq = [s for s in who if s == l] + [s for s in who if s != l]
         for n, s in enumerate(seq):
-            w, wr = weight(s)
+            if (s == l) != mine:
+                continue
+            wt, wr = weight(s, plus)
             for b in range(2):
-                buf, a = (srcb, zs[l // 2] * Z + l % 2 * H + 512 * b) if s == l else (landb, s * H + 512 * b)
+                buf, a = (srcb, z * Z + h * H + 512 * b) if s == l else (landb, s * w + d + 512 * b)
                 o = (bank + b) * 512
-                items.append((lambda o=o, w=w, buf=buf, a=a, st=n == 0, en=last and n == len(seq) - 1:
-                              PE.matmul(T.ps[:, o:o + 512], w, T[buf][:, a:a + 512], st, en),
+                items.append((lambda o=o, wt=wt, buf=buf, a=a, st=n == 0, en=n == len(seq) - 1:
+                              PE.matmul(T.ps[:, o:o + 512], wt, T[buf][:, a:a + 512], st, en),
                               [wr, R(buf, a, a + 512)], [R("ps", o, o + 512)]))
-        batch("t", items, acc=True)
+        if items:
+            batch("t", items, acc=True)
 
     def evac(dst, bank):
         for b in range(2):
             o = (bank + b) * 512
-            cp(T[dst][:, b * 512:b * 512 + 512], T.ps[:, o:o + 512], [R("ps", o, o + 512)], [R(dst, b * 512, b * 512 + 512)])
+            ts(T[dst][:, b * 512:b * 512 + 512], T.ps[:, o:o + 512], 1.0, None, OP.add, None, [R("ps", o, o + 512)], [R(dst, b * 512, b * 512 + 512)])
 
     def far_send(src, dst):
         h = l % 2
-        send(2 * far[l // 2] + 1, "r%s%d" % (dst, h), T[dst][:, h * H:(h + 1) * H], T[src][:], [R(src)])
+        send(C[2 * far[l // 2] + 1], "r%s%d" % (dst, h), T[dst][:, h * H:(h + 1) * H], T[src][:], [R(src)])
+
+    def far_p():
+        evac("fsp", 0)
+        if isA:
+            send(relay_of(core, T, topo), "rrelay", T.relay[:], T.fsp[:], [R("fsp")], off_es)
+        else:
+            far_send("fsp", "rfp")
+
+    def far_q():
+        evac("fsq", 2)
+        far_send("fsq", "rfq")
 
     def store(c0, c1):
         op("y", lambda: g.sync.dma_start(T.y[:, c0:c1], T.yo[:, c0:c1]), [R("yo", c0, c1)], [], True)
 
+    FP, FQ = (far, "xs", "lfp", hasP, 0), (far, qsrc, "lfq", hasQ, 2)
+    NP = (near, "xs", "lnp", hasP, 4)
+    solvers = [d for d in others if d % 2 == 1]
     if isA:
-        B = rank + 1
-        addup(far, "xs", "lfp", hasP, 0, True)
+        B = C[rank + 1]
+        cp(T.zeb[:], T.zin[:], [R("zin")], [R("zeb")])
+        scaled(6, "sb", "idh", lambda i: ("eb", i))
+        scaled(6, "sa", "idh", lambda i: ("ea", i))
+        ts(T.even[:], T.i4c[:], 0, None, OP.is_equal, None, [R("i4c")], [R("even")])
+        ts(T.bm[:], T.i3[:], T.kcol[:, 0:1], None, OP.is_equal, None, [R("i3"), R("kcol")], [R("bm")])
+        ts(T.wcol[:, 0:1], T.rmask[:, 0:1], 256.0, T.rmask[:, 1:2], OP.mult, OP.add, [R("rmask")], [R("wcol")])
+        ts(T.bev[:], T.i5[:], T.even[:, 0:1], None, OP.mult, None, [R("i5"), R("even")], [R("bev")])
+        ts(T.base[:], T.bm[:], T.wcol[:, 0:1], None, OP.mult, None, [R("bm"), R("wcol")], [R("base")])
+        batch("v", [(lambda b=b: V.tensor_scalar(T.iot[:, b * 256:(b + 1) * 256], T.il[:], T.odd[:, 0:1], T.bev[:, b:b + 1], OP.mult, OP.add),
+                     [R("il"), R("odd"), R("bev")], [R("iot", b * 256, (b + 1) * 256)]) for b in range(8)])
+        batch("s", [(lambda p=p: S.activation(T.zm[:, p:Z:16], T.zeb[:], COPY, scale=T.rmask[:, p:p + 1]),
+                     [R("zeb"), R("rmask")], [R("zm")]) for p in range(16)], acc=True)
+        batch("s", [(lambda r=r: S.activation(T.dd[:, r * 128 + r:(r + 1) * 128:16], T.base[:, r:128:16], COPY),
+                     [R("base")], [R("dd")]) for r in range(16)], acc=True)
+        for nm in ("na", "nb"):
+            op("s", lambda: S.activation(T[nm][:, Z:WZ], T.il[:], IDENT, scale=0.0, bias=8.0), [R("il")], [R(nm, Z, WZ)])
+        addup(*FP, True)
+        addup(*FQ, True)
         for nm, dst, o in (("sb", "lb", 2048), ("sa", "la", 2560)):
             items = []
             for i in range(6):
@@ -334,112 +389,120 @@ def rank_program(g, core, T, topo):
                               [R(nm, i * 128, (i + 1) * 128), R(buf, a, a + 128)], [R("ps", o, o + 128)]))
             batch("t", items, acc=True)
             cp(T[dst][:], T.ps[:, o:o + 128], [R("ps", o, o + 128)], [R(dst)])
-        addup(far, qsrc, "lfq", hasQ, 2, True)
-        for b in range(4):
-            o = 2048 + 512 * b
-            op("t", lambda: PE.matmul(T.ps[:, o:o + 512], T.bm[:], T.zm[:, b * 512:(b + 1) * 512], True, True),
-               [R("bm"), R("zm", b * 512, (b + 1) * 512)], [R("ps", o, o + 512)])
-
-        def scat(h):
-            cp(T.inv[:, 0:Z].indirect(T.lb[:, h * 64:(h + 1) * 64]), T.iot[:, h * H:(h + 1) * H], [R("lb"), R("iot")], [R("inv")])
-        scaled(16, "dd", "idh", lambda r: ("rmask", r))
-        scat(0)
-        evac("fsp", 0)
-        evac("fsq", 2)
-        far_send("fsp", "rfp")
-        far_send("fsq", "rfq")
         send(B, "rlb", T.lb[:], T.lb[:], [R("lb")])
-        addup(near, "xs", "lnp", hasP, 0, True)
-        addup(near, qsrc, "lnq", hasQ, 2, True)
-        scat(1)
-        for b in range(4):
-            o, c0, c1 = 2048 + 512 * b, 512 * b, 512 * b + 512
-            tt(T.invz[:, c0:c1], T.inv[:, c0:c1], T.ps[:, o:o + 512], OP.max, [R("inv", c0, c1), R("ps", o, o + 512)], [R("invz", c0, c1)])
+        if l in hasQ:
+            near_pieces(qsrc, "lnq", solvers, Z, all_es)
+        addup(*FP, False)
+        addup(*NP, True)
+        addup(*FQ, False)
 
-        def totable(hbuf, src, lst):
-            for h in range(2):
-                c0, c1, o = h * H, (h + 1) * H, 2048 + 512 * h
-                cp(T[hbuf][:, c0:c1], T[src][:, c0:c1], [R(src, c0, c1)], [R(hbuf, c0, c1)])
-                batch("t", [(lambda r=r: PE.matmul(T.ps[:, o:o + 64], T.dd[:, r * 128:(r + 1) * 128], T[hbuf][:, c0 + r:c1:16], r == 0, r == 15),
-                             [R("dd", r * 128, (r + 1) * 128), R(hbuf, c0, c1)], [R("ps", o, o + 64)]) for r in range(16)], acc=True)
-                cp(T[lst][:, h * 64:(h + 1) * 64], T.ps[:, o:o + 64], [R("ps", o, o + 64)], [R(lst, h * 64, (h + 1) * 64)])
+        def scat(i):
+            cp(T.inv[:, 0:Z].indirect(T.lb[:, i * 32:(i + 1) * 32]), T.iot[:, i * 512:(i + 1) * 512], [R("lb"), R("iot")], [R("inv")])
+        scat(0)
+        far_p()
+        scat(1)
+        scat(2)
+        far_q()
+        fill("bz", 0.0, 0, 128)
+        ts(T.bz[:, 0:128:2], T.bm[:, 0:128:2], 8.0, None, OP.mult, None, [R("bm")], [R("bz")])
+        fill("fi", 255)
+        scat(3)
+        addup(*NP, False)
+        for b in range(2):
+            o, c0 = 2048 + 512 * b, 512 * b
+            op("s", lambda: S.activation(T.nsp[:, c0:c0 + 512], T.ps[:, o:o + 512], COPY, scale=-1.0), [R("ps", o, o + 512)], [R("nsp", c0, c0 + 512)])
+        send(B, "rrnp", T.rnp[:], T.nsp[:], [R("nsp")])
+        for b in range(4):
+            c0, c1 = 512 * b, 512 * b + 512
+            op("t", lambda: PE.matmul(T.ps[:, c0:c1], T.bz[:], T.zm[:, c0:c1], True, True), [R("bz"), R("zm", c0, c1)], [R("ps", c0, c1)])
+            tt(T.invz[:, c0:c1], T.inv[:, c0:c1], T.ps[:, c0:c1], OP.max, [R("inv", c0, c1), R("ps", c0, c1)], [R("invz", c0, c1)])
+
+        def rows(src, h):
+            c0, c1, o = h * H, (h + 1) * H, 2048 + 512 * h
+            batch("t", [(lambda r=r: PE.matmul(T.ps[:, o:o + 64], T.dd[:, r * 128:(r + 1) * 128], T[src][:, c0 + r:c1:16], r == 0, r == 15),
+                         [R("dd"), R(src, c0, c1)], [R("ps", o, o + 64)]) for r in range(16)], acc=True)
+
+        def tab(lst, h):
+            o = 2048 + 512 * h
+            cp(T[lst][:, h * 64:(h + 1) * 64], T.ps[:, o:o + 64], [R("ps", o, o + 64)], [R(lst, h * 64, (h + 1) * 64)])
+
+        def give(lst):
+            send(B, "r" + lst, T[lst][:], T[lst][:], [R(lst)])
 
         for t in range(7):
-            w, old = ("wa", "wb")[t % 2], ("wb", "wa")[t % 2]
+            w, old = ("na", "nb")[t % 2], ("nb", "na")[t % 2]
             src, ww, lst = ("invz", Z, "la") if t == 0 else (old, WZ, "nl%d" % (t - 1))
-            for e, c, n in (("v", 0, 512), ("s", 512, 512), ("s", 1024, 1024)):
-                pick(e, w, c, src, 0, ww, lst, c // 16, n)
-            totable(("ha", "hb")[t % 2], w, "nl%d" % t)
-            send(B, "rnl%d" % t, T["nl%d" % t][:], T["nl%d" % t][:], [R("nl%d" % t)])
-            if t == 0:
-                evac("nsp", 0)
-                evac("nsq", 2)
-                send(B, "rrnp", T.rnp[:], T.nsp[:], [R("nsp")])
-                send(B, "rrnq", T.rnq[:], T.nsq[:], [R("nsq")])
-        totable("hb", "invz", "li")
-        send(B, "rli", T.li[:], T.li[:], [R("li")])
-        for c in range(2):
-            c0, c1 = c * H, (c + 1) * H
-            ts(T.fi[:, c0:c1], T.v7[:, 0:WZ].indirect(T.li[:, c * 64:(c + 1) * 64]), 255, None, OP.bitwise_and, None,
-               [R("v7"), R("li", c * 64, (c + 1) * 64)], [R("fi", c0, c1)])
-            cp(T.yo[:, c0:c1], T.fi[:, c0:c1], [R("fi", c0, c1)], [R("yo", c0, c1)])
+            for h in range(2):
+                if h == 1 and t > 0:
+                    tab(lst, 1)
+                    give(lst)
+                for e, c in (("v", h * H), ("s", h * H + 512)):
+                    pick(e, w, c, src, 0, ww, lst, c // 16, 512)
+                rows(w, h)
+            tab("nl%d" % t, 0)
+        tab("nl6", 1)
+        give("nl6")
+        for h in range(2):
+            rows("invz", h)
+            tab("li", h)
+        give("li")
+        for c0, c1 in CH:
+            ts(T.fi[:, c0:c1], T.v7[:, c0:c1], 255, None, OP.bitwise_and, None, [R("v7", c0, c1)], [R("fi", c0, c1)])
+        for c0, c1 in CH:
+            ts(T.yo[:, c0:c1], T.fi[:, 0:WZ].indirect(T.li[:, c0 // 16:c1 // 16]), -1.0, 255.0, OP.mult, OP.add,
+               [R("fi"), R("li", c0 // 16, c1 // 16)], [R("yo", c0, c1)])
             store(c0, c1)
     else:
-        addup(far, "xs", "lfp", hasP, 0, True)
-        addup(far, qsrc, "lfq", hasQ, 2, True)
-        evac("fsp", 0)
-        evac("fsq", 2)
-        far_send("fsp", "rfp")
-        far_send("fsq", "rfq")
-        addup(near, "xs", "lnp", hasP, 4, False)
-        addup(near, qsrc, "lnq", hasQ, 6, False)
+        if l in hasQ:
+            near_pieces(qsrc, "lnq", solvers, Z, all_es)
+        addup(*FP, True)
+        addup(*FQ, True)
+        addup(*NP, True, plus=False)
+        addup(*FP, False)
+        addup(near, qsrc, "lnq", hasQ, 6, True, 1)
+        addup(*FQ, False)
+        far_p()
+        far_q()
+        fill("v7", -1)
+        fill("wa", 0.0)
+        fill("wb", 0.0)
+        addup(*NP, False, plus=False)
+        addup(near, qsrc, "lnq", hasQ, 6, False, 1)
+        addup(near, qsrc, "lnq", hasQ, 2, True, 0)
+        addup(near, qsrc, "lnq", hasQ, 2, False, 0)
 
-        def more(buf, a, bank, st, en):
-            items = []
+        def settle(dst, h, add, a, bank, o):
             for b in range(2):
-                o, c = (bank + b) * 512, a + 512 * b
-                items.append((lambda o=o, c=c: PE.matmul(T.ps[:, o:o + 512], T.idh[:], T[buf][:, c:c + 512], st, en),
-                              [R("idh"), R(buf, c, c + 512)], [R("ps", o, o + 512)]))
-            batch("t", items, acc=True)
+                p, c0, d = (bank + b) * 512, h * H + 512 * b, a + 512 * b
+                tt(T[dst][:, c0:c0 + 512], T.ps[:, p:p + 512], T[add][:, d:d + 512], o,
+                   [R("ps", p, p + 512), R(add, d, d + 512)], [R(dst, c0, c0 + 512)])
 
-        def settle(dst, h, bank):
-            for b in range(2):
-                o, c0 = (bank + b) * 512, h * H + 512 * b
-                rd, wr = [R("ps", o, o + 512)], [R(dst, c0, c0 + 512)]
-                if h == 0:
-                    op("s", lambda: S.activation(T[dst][:, c0:c0 + 512], T.ps[:, o:o + 512], IDENT, bias=1.0), rd, wr)
-                else:
-                    ts(T[dst][:, c0:c0 + 512], T.ps[:, o:o + 512], 1.0, None, OP.add, None, rd, wr)
-
-        more("rnp", 0, 0, True, False)
-        more("rnq", 0, 2, True, False)
-        for fb, bank, dst in (("rfp", 0, "p1"), ("rfq", 2, "q1")):
-            for h in range(2):
-                more(fb, h * H, bank + 4 * h, False, True)
-                settle(dst, h, bank + 4 * h)
-
-        def comb(dst, win, ww, lst, add, c, o):
-            c0, c1 = c * H, (c + 1) * H
-            tt(T[dst][:, c0:c1], T[win][:, 0:ww].indirect(T[lst][:, c * 64:(c + 1) * 64]), T[add][:, c0:c1], o,
+        def comb(dst, win, ww, lst, add, c0, c1, o):
+            tt(T[dst][:, c0:c1], T[win][:, 0:ww].indirect(T[lst][:, c0 // 16:c1 // 16]), T[add][:, c0:c1], o,
                [R(win, 0, ww), R(lst), R(add, c0, c1)], [R(dst, c0, c1)])
 
+        settle("p1", 1, "rfp", H, 4, OP.subtract)
+        settle("q1", 1, "rfq", H, 6, OP.add)
+        for c0, c1 in ((0, 512), (512, H)):
+            tt(T.p1[:, c0:c1], T.rnp[:, c0:c1], T.rfp[:, c0:c1], OP.subtract, [R("rnp", c0, c1), R("rfp", c0, c1)], [R("p1", c0, c1)])
         for t in range(7):
             w, old = ("wa", "wb")[t % 2], ("wb", "wa")[t % 2]
-            for c in range(2):
+            for c0, c1 in ((H, Z), (0, H)):
                 if t == 0:
-                    comb(w, "p1", Z, "lb", "q1", c, OP.subtract)
+                    if c0 == 0:
+                        settle("q1", 0, "rfq", 0, 2, OP.add)
+                    comb(w, "p1", Z, "lb", "q1", c0, c1, OP.add)
                 else:
-                    comb(w, old, WZ, "nl%d" % (t - 1), "vc", c, OP.add)
-                c0, c1 = c * H, (c + 1) * H
-                op("s", lambda: S.activation(T.vc[:, c0:c1], T[w][:, c0:c1], COPY), [R(w, c0, c1)], [R("vc", c0, c1)])
-        for c in range(2):
-            c0, c1 = c * H, (c + 1) * H
-            comb("v7", "wa", WZ, "nl6", "vc", c, OP.add)
-            send(rank - 1, "rv%d" % c, T.v7[:, c0:c1], T.v7[:, c0:c1], [R("v7", c0, c1)])
-        for c in range(2):
-            c0, c1 = c * H, (c + 1) * H
-            comb("fi", "v7", WZ, "li", "p1", c, OP.subtract)
+                    comb(w, old, WZ, "nl%d" % (t - 1), "vc", c0, c1, OP.add)
+                op("s", lambda: S.activation(T.vc[:, c0:c1], T[w][:, c0:c1], IDENT, bias=-1.0 if t == 6 else 0.0), [R(w, c0, c1)], [R("vc", c0, c1)])
+        for c, (c0, c1) in enumerate(CH):
+            comb("v7", "wa", WZ, "nl6", "vc", c0, c1, OP.add)
+            send(C[rank - 1], "rv%d" % c, T.v7[:, c0:c1], T.v7[:, c0:c1], [R("v7", c0, c1)])
+        hs = ((0, H), (H, Z))
+        for c0, c1 in hs:
+            comb("fi", "v7", WZ, "li", "p1", c0, c1, OP.subtract)
+        for c0, c1 in hs:
             ts(T.fj[:, c0:c1], T.fi[:, c0:c1], 255, None, OP.bitwise_and, None, [R("fi", c0, c1)], [R("fj", c0, c1)])
-            ts(T.yo[:, c0:c1], T.fj[:, c0:c1], -1.0, 255.0, OP.mult, OP.add, [R("fj", c0, c1)], [R("yo", c0, c1)])
+            cp(T.yo[:, c0:c1], T.fj[:, c0:c1], [R("fj", c0, c1)], [R("yo", c0, c1)])
             store(c0, c1)
     finish(sent[0])

from concourse.bass import DstId, RemoteDMATransfer
from concourse.mybir import AluOpType, ActivationFunctionType

OP = AluOpType
COPY = ActivationFunctionType.Copy
IDENT = ActivationFunctionType.Identity
Z = 2048
H = 1024
WZ = Z + 256
NL = 90
LISTS = ["lb", "li"] + ["nl%d" % t for t in range(7)]
CH = ((1024, 2048), (0, 512), (512, 1024))

SCRATCH = {"ps": ("psum", [128, 4096], "float32")}
for _names, _cols, _dt in (
        ("xs qs", 4 * Z, "bfloat16"), ("lfp lfq lnp", 4 * H, "bfloat16"), ("lnq", 4 * Z, "bfloat16"),
        ("zm yo dd iot inv invz", Z, "bfloat16"),
        ("dm dp", 512, "bfloat16"), ("zeb bm bz base idb idn", 128, "bfloat16"), ("na nb", WZ, "bfloat16"), ("il", 256, "bfloat16"),
        ("pin", 512, "int32"), ("losti", 2, "int32"), ("zin i1 i3", 128, "int32"), ("i2 i2b", 16, "int32"),
        ("i4 i4b i4c", 4, "int32"), ("i5", 8, "int32"), ("v7 fi", WZ, "int32"), ("fj", Z, "int32"),
        ("lp", 512, "uint16"), (" ".join(LISTS) + " la", 128, "uint16"),
        ("ph", 512, "float16"), ("lpi sa sb", 768, "float16"), ("idh", 128, "float16"),
        ("rfp rfq", Z, "float16"), ("fsp fsq relay", H, "float16"), ("nsp rnp", H, "float32"),
        ("lostf", 2, "float32"), ("kcol odd even wcol", 4, "float32"), ("rmask", 16, "float32"), ("ea eb ms mn mp bev", 8, "float32"),
        ("p1 q1 vc", Z, "float32"), ("wa wb", WZ, "float32")):
    for _n in _names.split():
        SCRATCH[_n] = ("sbuf", [128, _cols], _dt)
SEMAPHORES = (["l%d" % i for i in range(NL)] + ["snt", "rpi", "rrelay"]
              + ["r%s%d" % (b, s) for b in ("lfp", "lfq", "lnp", "lnq") for s in range(4)]
              + ["rrfp0", "rrfp1", "rrfq0", "rrfq1", "rrnp", "rv0", "rv1", "rv2"] + ["r" + n for n in LISTS])


def tracker(g, T):
    E = {"g": g, "v": g.vector, "s": g.scalar, "t": g.tensor, "y": g.sync}
    known = {e: {} for e in E}
    count, waited, recs = {}, {}, {}
    free = ["l%d" % i for i in range(NL)]
    own = {e: [] for e in E}

    def wait(e, tok):
        sem, val, snap = tok
        k = known[e]
        if k.get(sem, 0) >= val:
            return
        E[e].wait_ge(T.sem[sem], val)
        waited[sem] = max(waited.get(sem, 0), val)
        k[sem] = val
        for s, n in snap.items():
            if k.get(s, 0) < n:
                k[s] = n

    def span(r):
        b, a, z = r
        return (b, a // 512 * 512, -(-z // 512) * 512) if b == "ps" else (b, a, z)

    def conflicts(who, reads, writes, acc):
        out = []
        for r in reads:
            b, a, z = span(r)
            for (x, y, kind, w, tok) in recs.get(b, []):
                if x < z and a < y and (kind == "w" or (b == "ps" and w != who)):
                    out.append(tok)
        for r in writes:
            b, a, z = span(r)
            for (x, y, kind, w, tok) in recs.get(b, []):
                if x < z and a < y and not (w == who and (kind == "r" or acc)):
                    out.append(tok)
        return out

    def note(reads, writes, who, tok):
        for r in writes:
            b, a, z = span(r)
            recs[b] = [q for q in recs.get(b, []) if not (a <= q[0] and q[1] <= z and q[4] is not tok)] + [(a, z, "w", who, tok)]
        for r in reads:
            b, a, z = span(r)
            recs.setdefault(b, []).append((a, z, "r", who, tok))

    def batch(e, items, dma=False, acc=False):
        who = "dma" if dma else e
        ins = []
        for fn, reads, writes in items:
            for t in sorted(conflicts(who, reads, writes, acc), key=lambda t: -len(t[2])):
                wait(e, t)
            ins.append(fn())
        done = [s for s in own[e] if known[e].get(s, 0) == count[s]]
        if not done:
            done = [free.pop(0)]
            own[e].append(done[0])
            count[done[0]] = 0
        sem = done[0]
        for i in ins:
            i.then_inc(T.sem[sem], 16 if dma else 1)
            count[sem] += 16 if dma else 1
        tok = (sem, count[sem], dict(known[e]))
        for fn, reads, writes in items:
            note(reads, writes, who, tok)

    def op(e, fn, reads, writes, dma=False):
        batch(e, [(fn, reads, writes)], dma)

    def landing(b, a, z, sem, val):
        count[sem] = val
        note([], [(b, a, z)], "remote", (sem, val, {}))

    def reading(e, reads):
        for t in conflicts(e, reads, [], False):
            wait(e, t)

    def finish(sent):
        count["snt"] = sent
        for s, n in count.items():
            if waited.get(s, 0) < n:
                g.wait_ge(T.sem[s], n)

    return op, batch, landing, reading, finish


def bits(es):
    return sum(1 << e for e in es)


def relay_of(core, T, topo):
    cs = topo.cores_of(core)
    same = [c for c in cs if T.rank_of(c) is not None and topo.die(c) == topo.die(core)]
    free = [c for c in cs if T.rank_of(c) is None and topo.die(c) != topo.die(core)]
    return free[same.index(core)]


def rank_program(g, core, T, topo):
    rank = T.rank_of(core)
    C = list(T.cores)
    if rank is None:
        for c in C[0::2]:
            if topo.chip(c) == topo.chip(core) and relay_of(c, T, topo) == core:
                here = [d for d in C if topo.chip(d) == topo.chip(c)]
                zs = [z for z in range(4) if C[2 * z] not in here]
                to = C[2 * zs[here.index(c) // 2] + 1]
                a = topo.addr(to)
                g.wait_ge(T.sem["rrelay"], len(topo.engines(c, to)))
                g.remote_dma(out_ap=T.rfp[:, 0:H], in_ap=T.relay[:], remote_sem=T.sem["rrfp0"],
                             local_sem=T.sem["snt"], pid=a[1], routing_id=a[0], dma_engine_mask=topo.mask(core, to))
                g.wait_ge(T.sem["snt"], len(topo.engines(core, to)))
        return
    V, S, PE = g.vector, g.scalar, g.tensor
    op, batch, landing, reading, finish = tracker(g, T)
    local = [r for r in range(8) if topo.chip(C[r]) == topo.chip(core)]
    l = local.index(rank)
    near = sorted({r // 2 for r in local})
    far = [z for z in range(4) if z not in near]
    isA = rank % 2 == 0
    zone = rank // 2
    data = rank < 6
    hasP = [s for s in range(4) if local[s] != 7]
    hasQ = [s for s in range(4) if local[s] != 6]
    others = [d for d in range(4) if d != l]
    away = [r for r in range(8) if r not in local]
    all_es = topo.engines(core, C[local[others[0]]])
    off_es = topo.engines(core, C[away[0]])
    on_es = [e for e in all_es if e not in off_es]
    sent = [0]

    def R(b, a=0, z=None):
        return (b, a, SCRATCH[b][1][1] if z is None else z)

    def send(to, sem, dst, src, reads, es=None):
        reading("g", reads)
        a = topo.addr(to)
        es = topo.engines(core, to) if es is None else es
        g.remote_dma(out_ap=dst, in_ap=src, remote_sem=T.sem[sem], local_sem=T.sem["snt"], pid=a[1], routing_id=a[0],
                     dma_engine_mask=bits(es))
        sent[0] += len(es)

    def send_all(parts, reads):
        reading("g", reads)
        trs = []
        for r, sem, dst, src, es in parts:
            a = topo.addr(C[r])
            trs.append(RemoteDMATransfer(dst_ids=[DstId(rid=a[0], pnc=a[1])], dma_engine_mask=bits(es),
                                         remote_sem=T.sem[sem], src=src, dst=dst))
            sent[0] += len(es)
        g.remote_dma_fused(trs, local_sem=T.sem["snt"])

    def width(r):
        return len(topo.engines(C[r], core))
    for b, who, w, n in (("lfp", hasP, H, 4), ("lfq", hasQ, H, 4), ("lnp", hasP, H, len(on_es)), ("lnq", hasQ, Z, len(all_es))):
        for s in who:
            if s != l and not (isA and b == "lnq"):
                landing(b, s * w, (s + 1) * w, "r%s%d" % (b, s), n)
    if isA:
        landing("lpi", 0, 768, "rpi", 4 * (5 if data else 6))
        for c, (c0, c1) in enumerate(CH):
            landing("v7", c0, c1, "rv%d" % c, width(rank + 1))
    else:
        for n in LISTS:
            landing(n, 0, 128, "r" + n, width(rank - 1))
        landing("rnp", 0, H, "rrnp", width(rank - 1))
        for b in ("rfp", "rfq"):
            for h in range(2):
                landing(b, h * H, (h + 1) * H, "r%s%d" % (b, h), width(away[0]))

    def load(e, dst, src, w):
        q = g.sync if e == "y" else S
        op(e, lambda: q.dma_start(dst, src), [], [w], True)

    def loadx(e, z):
        load(e, T.xs[:, z * Z:(z + 1) * Z], T.x[:, z * Z:(z + 1) * Z], R("xs", z * Z, (z + 1) * Z))
    mine_first = sorted(near, key=lambda z: z != zone)
    if data:
        load("y", T.pin[:], T.pi[:], R("pin"))
    load("s", T.losti[:], T.lost[:], R("losti"))
    if isA:
        load("s", T.zin[:], T.zero[:], R("zin"))
    loadx("y", far[0])
    loadx("s", far[1])
    for z in mine_first:
        loadx("y", z)

    def iota(b, pattern, base, cm, **kw):
        op("g", lambda: g.iota(T[b][:], pattern, base, cm, **kw), [], [R(b)])
    iota("i1", [[-1, 128]], 0, 1)
    iota("i5", [[1, 8]], 0, 0)
    if isA:
        iota("i2", [[-1, 16]], 16, 1)
        iota("i3", [[1, 8], [0, 16]], 0, 0)
        iota("i4", [[0, 4]], 0, 1)
        iota("il", [[1, 256]], 0, 0, allow_small_or_imprecise_dtypes=True)

    def ts(out, in0, s1, s2, op0, op1, reads, writes):
        a = (out, in0, s1, s2, op0) if op1 is None else (out, in0, s1, s2, op0, op1)
        op("v", lambda: V.tensor_scalar(*a), reads, writes)

    def tt(out, in0, in1, o, reads, writes):
        op("v", lambda: V.tensor_tensor(out, in0, in1, o), reads, writes)

    def cp(out, in_, reads, writes):
        op("v", lambda: V.tensor_copy(out, in_), reads, writes)

    def fill(b, c, a=Z, z=WZ):
        op("v", lambda: V.memset(T[b][:, a:z], c), [], [(b, a, z)])

    def scaled(n, dst, idn, col):
        items = []
        for i in range(n):
            b, j = col(i)
            items.append((lambda i=i, b=b, j=j: V.tensor_scalar(T[dst][:, i * 128:(i + 1) * 128], T[idn][:], T[b][:, j:j + 1], None, OP.mult),
                          [R(idn), R(b)], [R(dst, i * 128, (i + 1) * 128)]))
        batch("v", items)

    if isA:
        fill("dd", 0.0, 0, Z)
    ts(T.idb[:], T.i1[:], 0, None, OP.is_equal, None, [R("i1")], [R("idb")])
    if isA:
        ts(T.idh[:], T.i1[:], 0, None, OP.is_equal, None, [R("i1")], [R("idh")])
        ts(T.i2b[:], T.i2[:], 15, None, OP.bitwise_and, None, [R("i2")], [R("i2b")])
        ts(T.i4b[:], T.i4[:], 4, None, OP.arith_shift_right, None, [R("i4")], [R("i4b")])
        ts(T.i4c[:], T.i4[:], 1, None, OP.bitwise_and, None, [R("i4")], [R("i4c")])
        ts(T.rmask[:], T.i2b[:], 0, None, OP.is_equal, None, [R("i2b")], [R("rmask")])
        cp(T.kcol[:], T.i4b[:], [R("i4b")], [R("kcol")])
        cp(T.odd[:], T.i4c[:], [R("i4c")], [R("odd")])
    if data:
        cp(T.ph[:], T.pin[:], [R("pin")], [R("ph")])
        where = [(2 * z, off_es[4 * i:4 * i + 4]) for i, z in enumerate(far)]
        where += [(r, on_es[4 * i:4 * i + 4]) for i, r in enumerate(2 * z for z in near if 2 * z != rank)]
        send_all([(r, "rpi", T.lpi[:, rank * 128:(rank + 1) * 128], T.ph[:, (r // 2) * 128:(r // 2 + 1) * 128], es)
                  for r, es in where], [R("ph")])
        cp(T.lp[:], T.pin[:], [R("pin")], [R("lp")])
    cp(T.lostf[:], T.losti[:], [R("losti")], [R("lostf")])
    ts(T.ea[:], T.i5[:], T.lostf[:, 0:1], None, OP.is_equal, None, [R("i5"), R("lostf")], [R("ea")])
    ts(T.eb[:], T.i5[:], T.lostf[:, 1:2], None, OP.is_equal, None, [R("i5"), R("lostf")], [R("eb")])
    tt(T.ms[:], T.ea[:], T.eb[:], OP.add, [R("ea"), R("eb")], [R("ms")])
    ts(T.mn[:], T.ms[:], -1.0, None, OP.add, None, [R("ms")], [R("mn")])
    nd = len([r for r in local if r < 6])
    scaled(nd, "dm", "idb", lambda i: ("mn", local[i]))

    def weight(s, plus):
        m, i = ("dm", "idb") if plus else ("dp", "idn")
        return (T[m][:, s * 128:(s + 1) * 128], R(m, s * 128, (s + 1) * 128)) if local[s] < 6 else (T[i][:], R(i))

    def pick(e, dst, d0, src, s0, s1, lst, t0, n):
        out, in_ = T[dst][:, d0:d0 + n], T[src][:, s0:s1].indirect(T[lst][:, t0:t0 + n // 16])
        rd, wr = [R(src, s0, s1), R(lst, t0, t0 + n // 16)], [R(dst, d0, d0 + n)]
        if e == "v":
            op("v", lambda: V.tensor_copy(out, in_), rd, wr)
        else:
            op("s", lambda: S.activation(out, in_, COPY), rd, wr)

    def gather(e, z):
        pick(e, "qs", z * Z, "xs", z * Z, (z + 1) * Z, "lp", z * 128, Z)

    def piece(zs, srcb, landb, d, w, es):
        a = zs[d // 2] * Z + (d % 2 * H if w == H else 0)
        return (local[d], "r%s%d" % (landb, l), T[landb][:, l * w:(l + 1) * w], T[srcb][:, a:a + w], es), R(srcb, a, a + w)

    def far_pieces(srcb, landb):
        ps = [piece(far, srcb, landb, d, H, topo.engines(core, C[local[d]])[4 * i:4 * i + 4]) for i, d in enumerate(others)]
        send_all([p[0] for p in ps], [p[1] for p in ps])

    def near_pieces(srcb, landb, to, w, es):
        for d in sorted(to, key=lambda d: d // 2 != l // 2):
            (r, sem, dst, src, es), rd = piece(near, srcb, landb, d, w, es)
            send(C[r], sem, dst, src, [rd], es)

    qsrc = "qs" if data else "xs"
    if data:
        gather("v", far[0])
        gather("s", far[1])
    if l in hasP:
        far_pieces("xs", "lfp")
    if l in hasQ:
        far_pieces(qsrc, "lfq")
    if l in hasP:
        near_pieces("xs", "lnp", others, H, on_es)
    if not isA:
        ts(T.mp[:], T.mn[:], -1.0, None, OP.mult, None, [R("mn")], [R("mp")])
        scaled(nd, "dp", "idb", lambda i: ("mp", local[i]))
        ts(T.idn[:], T.idb[:], -1.0, None, OP.mult, None, [R("idb")], [R("idn")])
    if data:
        gather("s", mine_first[0])
        gather("s" if isA else "v", mine_first[1])

    def addup(zs, srcb, landb, who, bank, mine, half=None, plus=True):
        items = []
        z, w, d, h = (zs[l // 2], H, 0, l % 2) if half is None else (zone, Z, half * H, half)
        seq = [s for s in who if s == l] + [s for s in who if s != l]
        for n, s in enumerate(seq):
            if (s == l) != mine:
                continue
            wt, wr = weight(s, plus)
            for b in range(2):
                buf, a = (srcb, z * Z + h * H + 512 * b) if s == l else (landb, s * w + d + 512 * b)
                o = (bank + b) * 512
                items.append((lambda o=o, wt=wt, buf=buf, a=a, st=n == 0, en=n == len(seq) - 1:
                              PE.matmul(T.ps[:, o:o + 512], wt, T[buf][:, a:a + 512], st, en),
                              [wr, R(buf, a, a + 512)], [R("ps", o, o + 512)]))
        if items:
            batch("t", items, acc=True)

    def evac(dst, bank):
        for b in range(2):
            o = (bank + b) * 512
            ts(T[dst][:, b * 512:b * 512 + 512], T.ps[:, o:o + 512], 1.0, None, OP.add, None, [R("ps", o, o + 512)], [R(dst, b * 512, b * 512 + 512)])

    def far_send(src, dst):
        h = l % 2
        send(C[2 * far[l // 2] + 1], "r%s%d" % (dst, h), T[dst][:, h * H:(h + 1) * H], T[src][:], [R(src)])

    def far_p():
        evac("fsp", 0)
        if isA:
            send(relay_of(core, T, topo), "rrelay", T.relay[:], T.fsp[:], [R("fsp")], off_es)
        else:
            far_send("fsp", "rfp")

    def far_q():
        evac("fsq", 2)
        far_send("fsq", "rfq")

    def store(c0, c1):
        op("y", lambda: g.sync.dma_start(T.y[:, c0:c1], T.yo[:, c0:c1]), [R("yo", c0, c1)], [], True)

    FP, FQ = (far, "xs", "lfp", hasP, 0), (far, qsrc, "lfq", hasQ, 2)
    NP = (near, "xs", "lnp", hasP, 4)
    solvers = [d for d in others if d % 2 == 1]
    if isA:
        B = C[rank + 1]
        cp(T.zeb[:], T.zin[:], [R("zin")], [R("zeb")])
        scaled(6, "sb", "idh", lambda i: ("eb", i))
        scaled(6, "sa", "idh", lambda i: ("ea", i))
        ts(T.even[:], T.i4c[:], 0, None, OP.is_equal, None, [R("i4c")], [R("even")])
        ts(T.bm[:], T.i3[:], T.kcol[:, 0:1], None, OP.is_equal, None, [R("i3"), R("kcol")], [R("bm")])
        ts(T.wcol[:, 0:1], T.rmask[:, 0:1], 256.0, T.rmask[:, 1:2], OP.mult, OP.add, [R("rmask")], [R("wcol")])
        ts(T.bev[:], T.i5[:], T.even[:, 0:1], None, OP.mult, None, [R("i5"), R("even")], [R("bev")])
        ts(T.base[:], T.bm[:], T.wcol[:, 0:1], None, OP.mult, None, [R("bm"), R("wcol")], [R("base")])
        batch("v", [(lambda b=b: V.tensor_scalar(T.iot[:, b * 256:(b + 1) * 256], T.il[:], T.odd[:, 0:1], T.bev[:, b:b + 1], OP.mult, OP.add),
                     [R("il"), R("odd"), R("bev")], [R("iot", b * 256, (b + 1) * 256)]) for b in range(8)])
        batch("s", [(lambda p=p: S.activation(T.zm[:, p:Z:16], T.zeb[:], COPY, scale=T.rmask[:, p:p + 1]),
                     [R("zeb"), R("rmask")], [R("zm")]) for p in range(16)], acc=True)
        batch("s", [(lambda r=r: S.activation(T.dd[:, r * 128 + r:(r + 1) * 128:16], T.base[:, r:128:16], COPY),
                     [R("base")], [R("dd")]) for r in range(16)], acc=True)
        for nm in ("na", "nb"):
            op("s", lambda: S.activation(T[nm][:, Z:WZ], T.il[:], IDENT, scale=0.0, bias=8.0), [R("il")], [R(nm, Z, WZ)])
        addup(*FP, True)
        addup(*FQ, True)
        for nm, dst, o in (("sb", "lb", 2048), ("sa", "la", 2560)):
            items = []
            for i in range(6):
                buf, a = ("ph", zone * 128) if i == rank else ("lpi", i * 128)
                items.append((lambda i=i, buf=buf, a=a: PE.matmul(T.ps[:, o:o + 128], T[nm][:, i * 128:(i + 1) * 128], T[buf][:, a:a + 128], i == 0, i == 5),
                              [R(nm, i * 128, (i + 1) * 128), R(buf, a, a + 128)], [R("ps", o, o + 128)]))
            batch("t", items, acc=True)
            cp(T[dst][:], T.ps[:, o:o + 128], [R("ps", o, o + 128)], [R(dst)])
        send(B, "rlb", T.lb[:], T.lb[:], [R("lb")])
        if l in hasQ:
            near_pieces(qsrc, "lnq", solvers, Z, all_es)
        addup(*FP, False)
        addup(*NP, True)
        addup(*FQ, False)

        def scat(i):
            cp(T.inv[:, 0:Z].indirect(T.lb[:, i * 32:(i + 1) * 32]), T.iot[:, i * 512:(i + 1) * 512], [R("lb"), R("iot")], [R("inv")])
        scat(0)
        far_p()
        scat(1)
        scat(2)
        far_q()
        fill("bz", 0.0, 0, 128)
        ts(T.bz[:, 0:128:2], T.bm[:, 0:128:2], 8.0, None, OP.mult, None, [R("bm")], [R("bz")])
        fill("fi", 255)
        scat(3)
        addup(*NP, False)
        for b in range(2):
            o, c0 = 2048 + 512 * b, 512 * b
            op("s", lambda: S.activation(T.nsp[:, c0:c0 + 512], T.ps[:, o:o + 512], COPY, scale=-1.0), [R("ps", o, o + 512)], [R("nsp", c0, c0 + 512)])
        send(B, "rrnp", T.rnp[:], T.nsp[:], [R("nsp")])
        for b in range(4):
            c0, c1 = 512 * b, 512 * b + 512
            op("t", lambda: PE.matmul(T.ps[:, c0:c1], T.bz[:], T.zm[:, c0:c1], True, True), [R("bz"), R("zm", c0, c1)], [R("ps", c0, c1)])
            tt(T.invz[:, c0:c1], T.inv[:, c0:c1], T.ps[:, c0:c1], OP.max, [R("inv", c0, c1), R("ps", c0, c1)], [R("invz", c0, c1)])

        def rows(src, h):
            c0, c1, o = h * H, (h + 1) * H, 2048 + 512 * h
            batch("t", [(lambda r=r: PE.matmul(T.ps[:, o:o + 64], T.dd[:, r * 128:(r + 1) * 128], T[src][:, c0 + r:c1:16], r == 0, r == 15),
                         [R("dd"), R(src, c0, c1)], [R("ps", o, o + 64)]) for r in range(16)], acc=True)

        def tab(lst, h):
            o = 2048 + 512 * h
            cp(T[lst][:, h * 64:(h + 1) * 64], T.ps[:, o:o + 64], [R("ps", o, o + 64)], [R(lst, h * 64, (h + 1) * 64)])

        def give(lst):
            send(B, "r" + lst, T[lst][:], T[lst][:], [R(lst)])

        for t in range(7):
            w, old = ("na", "nb")[t % 2], ("nb", "na")[t % 2]
            src, ww, lst = ("invz", Z, "la") if t == 0 else (old, WZ, "nl%d" % (t - 1))
            for h in range(2):
                if h == 1 and t > 0:
                    tab(lst, 1)
                    give(lst)
                for e, c in (("v", h * H), ("s", h * H + 512)):
                    pick(e, w, c, src, 0, ww, lst, c // 16, 512)
                rows(w, h)
            tab("nl%d" % t, 0)
        tab("nl6", 1)
        give("nl6")
        for h in range(2):
            rows("invz", h)
            tab("li", h)
        give("li")
        for c0, c1 in CH:
            ts(T.fi[:, c0:c1], T.v7[:, c0:c1], 255, None, OP.bitwise_and, None, [R("v7", c0, c1)], [R("fi", c0, c1)])
        for c0, c1 in CH:
            ts(T.yo[:, c0:c1], T.fi[:, 0:WZ].indirect(T.li[:, c0 // 16:c1 // 16]), -1.0, 255.0, OP.mult, OP.add,
               [R("fi"), R("li", c0 // 16, c1 // 16)], [R("yo", c0, c1)])
            store(c0, c1)
    else:
        if l in hasQ:
            near_pieces(qsrc, "lnq", solvers, Z, all_es)
        addup(*FP, True)
        addup(*FQ, True)
        addup(*NP, True, plus=False)
        addup(*FP, False)
        addup(near, qsrc, "lnq", hasQ, 6, True, 1)
        addup(*FQ, False)
        far_p()
        far_q()
        fill("v7", -1)
        fill("wa", 0.0)
        fill("wb", 0.0)
        addup(*NP, False, plus=False)
        addup(near, qsrc, "lnq", hasQ, 6, False, 1)
        addup(near, qsrc, "lnq", hasQ, 2, True, 0)
        addup(near, qsrc, "lnq", hasQ, 2, False, 0)

        def settle(dst, h, add, a, bank, o):
            for b in range(2):
                p, c0, d = (bank + b) * 512, h * H + 512 * b, a + 512 * b
                tt(T[dst][:, c0:c0 + 512], T.ps[:, p:p + 512], T[add][:, d:d + 512], o,
                   [R("ps", p, p + 512), R(add, d, d + 512)], [R(dst, c0, c0 + 512)])

        def comb(dst, win, ww, lst, add, c0, c1, o):
            tt(T[dst][:, c0:c1], T[win][:, 0:ww].indirect(T[lst][:, c0 // 16:c1 // 16]), T[add][:, c0:c1], o,
               [R(win, 0, ww), R(lst), R(add, c0, c1)], [R(dst, c0, c1)])

        settle("p1", 1, "rfp", H, 4, OP.subtract)
        settle("q1", 1, "rfq", H, 6, OP.add)
        for c0, c1 in ((0, 512), (512, H)):
            tt(T.p1[:, c0:c1], T.rnp[:, c0:c1], T.rfp[:, c0:c1], OP.subtract, [R("rnp", c0, c1), R("rfp", c0, c1)], [R("p1", c0, c1)])
        for t in range(7):
            w, old = ("wa", "wb")[t % 2], ("wb", "wa")[t % 2]
            for c0, c1 in ((H, Z), (0, H)):
                if t == 0:
                    if c0 == 0:
                        settle("q1", 0, "rfq", 0, 2, OP.add)
                    comb(w, "p1", Z, "lb", "q1", c0, c1, OP.add)
                else:
                    comb(w, old, WZ, "nl%d" % (t - 1), "vc", c0, c1, OP.add)
                op("s", lambda: S.activation(T.vc[:, c0:c1], T[w][:, c0:c1], IDENT, bias=-1.0 if t == 6 else 0.0), [R(w, c0, c1)], [R("vc", c0, c1)])
        for c, (c0, c1) in enumerate(CH):
            comb("v7", "wa", WZ, "nl6", "vc", c0, c1, OP.add)
            send(C[rank - 1], "rv%d" % c, T.v7[:, c0:c1], T.v7[:, c0:c1], [R("v7", c0, c1)])
        hs = ((0, H), (H, Z))
        for c0, c1 in hs:
            comb("fi", "v7", WZ, "li", "p1", c0, c1, OP.subtract)
        for c0, c1 in hs:
            ts(T.fj[:, c0:c1], T.fi[:, c0:c1], 255, None, OP.bitwise_and, None, [R("fi", c0, c1)], [R("fj", c0, c1)])
            cp(T.yo[:, c0:c1], T.fj[:, c0:c1], [R("fj", c0, c1)], [R("yo", c0, c1)])
            store(c0, c1)
    finish(sent[0])
